import numpy as np, ml_dtypes
CORES = [23,39,55,63,87,103,111,127,18,34,50,58,82,98,106,122]
N = 16
GR, GC = 4, 4
L, KA, KB, F = 4, 1, 1, 32
def setup_inputs(rng):
    return {"a": rng.standard_normal((N, 128, KA * 128), dtype=np.float32).astype(ml_dtypes.bfloat16), "b": rng.standard_normal((N, 128, KB * F), dtype=np.float32).astype(ml_dtypes.bfloat16)}
def reference(a, b):
    A, B = a.astype(np.float64), b.astype(np.float64)
    y = np.zeros((N, 128, F))
    for i in range(GR):
        for j in range(GC):
            for k in range(L):
                At = A[i * GC + k // KA][:, 128 * (k % KA):128 * (k % KA) + 128]
                Bt = B[(k // KB) * GC + j][:, F * (k % KB):F * (k % KB) + F]
                y[i * GC + j] += At.T @ Bt
    return {"y": y.astype(ml_dtypes.bfloat16 if a.dtype != np.float64 else np.float64)}

from concourse.bass import DstId, RemoteDMATransfer

GR, GC = 4, 4

SCRATCH = {
    "astk": ("dram", [4, 128, 128], "bfloat16"),
    "bstk": ("dram", [4, 128, 32], "bfloat16"),
    "asb": ("sbuf", [128, 512], "bfloat16"),
    "bsb": ("sbuf", [128, 128], "bfloat16"),
    "acc": ("psum", [128, 32], "float32"),
    "ysb": ("sbuf", [128, 32], "bfloat16"),
}
SEMAPHORES = ["lda", "ldb", "arra", "arrb", "sent", "gota", "gotb", "mm", "cp", "st"]


def _row_peers(r):
    return [(r // GC) * GC + k for k in range(GC) if k != r % GC]


def _col_peers(r):
    return [k * GC + r % GC for k in range(GR) if k != r // GC]


def _mask(topo, cores, r, peers):
    m = None
    for p in peers:
        if not topo.may_write(cores[r], cores[p]):
            raise ValueError("rank %d may not write to rank %d" % (r, p))
        mm = topo.mask(cores[r], cores[p])
        m = mm if m is None else (m & mm)
    return m


def _engines(m):
    return bin(m).count("1")


def rank_program(g, core, T, topo):
    r = T.rank_of(core)
    if r is None:
        return
    cores = T.cores
    i, j = r // GC, r % GC
    S = T.sem

    g.sync.dma_start(T.astk[j], T.a[:]).then_inc(S.lda, 16)
    g.scalar.dma_start(T.bstk[i], T.b[:]).then_inc(S.ldb, 16)

    def send(peers, src, sem):
        ids = []
        for p in peers:
            rid, pid, _se = topo.addr(cores[p])
            ids.append(DstId(rid=rid, pnc=pid))
        m = _mask(topo, cores, r, peers)
        g.remote_dma_fused(
            [RemoteDMATransfer(dst_ids=ids, dma_engine_mask=m, remote_sem=sem, srcs=[src],
                               dsts=[src for _p in peers], alu_op=0)],
            local_sem=S.sent)
        return _engines(m)

    g.wait_ge(S.lda, 16)
    left = send(_row_peers(r), T.astk[j], S.arra)
    g.wait_ge(S.ldb, 16)
    left += send(_col_peers(r), T.bstk[i], S.arrb)

    need_a = sum(_engines(_mask(topo, cores, p, _row_peers(p))) for p in _row_peers(r))
    need_b = sum(_engines(_mask(topo, cores, p, _col_peers(p))) for p in _col_peers(r))
    g.sync.wait_ge(S.lda, 16)
    g.sync.wait_ge(S.arra, need_a)
    g.sync.dma_start(T.asb[:], T.astk[:]).then_inc(S.gota, 16)
    g.scalar.wait_ge(S.ldb, 16)
    g.scalar.wait_ge(S.arrb, need_b)
    g.scalar.dma_start(T.bsb[:], T.bstk[:]).then_inc(S.gotb, 16)

    g.tensor.wait_ge(S.gotb, 16)
    g.tensor.wait_ge(S.gota, 16)
    for u in range(4):
        mmi = g.tensor.matmul(T.acc[:], T.asb[:, 128 * u:128 * (u + 1)], T.bsb[:, 32 * u:32 * (u + 1)],
                              u == 0, u == 3)
    mmi.then_inc(S.mm, 1)
    g.vector.wait_ge(S.mm, 1)
    g.vector.tensor_copy(T.ysb[:], T.acc[:]).then_inc(S.cp, 1)
    g.sync.wait_ge(S.cp, 1)
    g.sync.dma_start(T.y[:], T.ysb[:]).then_inc(S.st, 16)
    g.sync.wait_ge(S.st, 16)

    g.wait_ge(S.sent, left)
